import numpy as np
import ml_dtypes


def mxq(x, axis, fmt="e4m3"):
    dtype, down = {"e4m3": (ml_dtypes.float8_e4m3fn, 7), "e5m2": (ml_dtypes.float8_e5m2, 14)}[fmt]
    v = np.moveaxis(np.asarray(x, np.float32).astype(ml_dtypes.bfloat16).astype(np.float64), axis, -1)
    blocks = v.reshape(v.shape[:-1] + (-1, 32))
    amax = np.abs(blocks).max(-1, keepdims=True)
    byte = np.maximum(np.where(amax > 0, np.frexp(amax)[1] - 1 + 127, 0) - down, 1)
    scale = np.exp2(byte - 127.0)
    codes = (blocks / scale).astype(np.float32).astype(dtype).astype(np.float64)
    return np.moveaxis((codes * scale).reshape(v.shape), -1, axis)


WIDE = False


def mx_kscale(k):
    if not WIDE:
        return np.ones(k)
    levels = np.array([10, -10, 5, -5, 0])
    if k % 512:
        return np.exp2(np.random.permutation(np.resize(levels, k // 32))).repeat(32)
    a = np.empty((k // 512, 16))
    for p in range(k // 512):
        a[p, :8] = np.random.permutation(np.resize(levels, 8))
        for g in range(8):
            far = levels[np.abs(levels - a[p, g]) >= 10]
            a[p, g + 8] = far[np.random.randint(len(far))]
    return np.exp2(a.ravel()).repeat(32)


def f64(x):
    return np.asarray(x).astype(np.float64)


def striped(idx):
    return np.tile(idx.reshape(-1, 16).T, (8, 1)).astype(np.uint16)


def unstriped(offs):
    return offs[:16].T.reshape(-1).astype(np.int64)


E2M1 = np.array([0.0, 0.5, 1.0, 1.5, 2.0, 3.0, 4.0, 6.0, -0.0, -0.5, -1.0, -1.5, -2.0, -3.0, -4.0, -6.0])


def pack_weight(w, fmt):
    k, n = w.shape
    w = f64(np.asarray(w, np.float32).astype(ml_dtypes.bfloat16)).reshape(k // 32, 32, n)
    amax = np.abs(w).max(1)
    if fmt == "e4m3":
        byte = np.frexp(amax)[1] - 1 + 127 - 7
    else:
        mant, ex = np.frexp(amax / 6.0)
        byte = np.where(mant > 0.5, ex, ex - 1) + 127
    byte = np.clip(np.where(amax > 0, byte, 1), 1, 254)
    scaled = (w * np.exp2(127.0 - byte)[:, None, :]).reshape(k, n).astype(np.float32)
    by_word = np.ascontiguousarray(scaled.reshape(k // 512, 128, 4, n).transpose(0, 1, 3, 2))
    if fmt == "e4m3":
        words = by_word.astype(ml_dtypes.float8_e4m3fn).view(np.uint8)
    else:
        c = by_word.astype(ml_dtypes.float4_e2m1fn).view(np.uint8) & 0xF
        words = (c[..., 0::2] | (c[..., 1::2] << 4)).reshape(k // 512, 128, 2 * n)
    return np.ascontiguousarray(words), np.ascontiguousarray(byte.astype(np.uint8).reshape(k // 512, 16, n))


def unpack_weight(words, scales, fmt):
    g, _, n = scales.shape
    words = np.ascontiguousarray(words).reshape(g, 128, n, -1)
    if fmt == "e4m3":
        vals = words.view(ml_dtypes.float8_e4m3fn).astype(np.float64)
    else:
        nib = np.empty((g, 128, n, 4), np.uint8)
        nib[..., 0::2] = words & 0xF
        nib[..., 1::2] = words >> 4
        vals = E2M1[nib]
    vals = vals * np.repeat(np.exp2(scales.astype(np.float64) - 127.0), 8, axis=1)[..., None]
    return vals.transpose(0, 1, 3, 2).reshape(g * 512, n)


def gelu(v):
    return 0.5 * v * (1.0 + np.tanh(np.sqrt(2.0 / np.pi) * (v + 0.044715 * v**3)))


K, H, T, S, T2, P = 1536, 1024, 2048, 512, 1024, 512

def setup_inputs():
    n = np.random.standard_normal
    s = mx_kscale(K)[:, None]
    u = mx_kscale(H)[:, None]
    d = {}
    d["tab_words"], d["tab_scales"] = pack_weight(n((K, T)) * s, "e4m3")
    d["w1"] = (n((K, H)) / K**0.5 / s * u.T).astype(np.float32)
    d["w4_words"], d["w4_scales"] = pack_weight(n((K, H)) / K**0.5 / s * u.T, "e2m1")
    d["page0"] = (n((H, T2)) * u).astype(np.float32)
    d["wgs"] = np.exp(0.3 * n((128, S))).astype(np.float32)
    d["low"] = (0.7 * n(H) * u[:, 0]).astype(np.float32)
    d["rate"] = (1.5 * n(H) / H**0.5 / u[:, 0]**2).astype(np.float32)
    d["course"] = (1.2 * n((H, P)) / H**0.5 / u).astype(np.float32)
    d["slot"] = np.exp(0.5 * n(T2)).astype(np.float32)
    d["offs"] = striped(np.random.permutation(T)[:S])
    d["offs2"] = striped(np.random.permutation(T2)[:S])
    d["offs3"] = striped(np.random.permutation(T2)[:P])
    return d

def reference(tab_words, tab_scales, w1, w4_words, w4_scales, page0, wgs, low, rate, course, slot, offs, offs2, offs3):
    v = unpack_weight(tab_words, tab_scales, "e4m3")[:, unstriped(offs)]
    w4 = unpack_weight(w4_words, w4_scales, "e2m1")
    a = mxq(f64(w1), 0, "e4m3").T @ v
    b = w4.T @ v
    h = a + np.abs(b)
    page = f64(page0).copy()
    page[:, unstriped(offs2)] = np.tile(f64(wgs), (H // 128, 1)) * h
    x = np.maximum(page[:, unstriped(offs3)], f64(low)[:, None]) * f64(rate)[:, None]
    pq = mxq(page, 0, "e4m3")
    e = pq.T @ mxq(x, 0, "e4m3")
    f = pq.T @ mxq(f64(course), 0, "e4m3")
    return f64(slot)[:, None] * e / (1.0 + np.abs(f))

@@ -1,0 +1,365 @@
+from contextlib import ExitStack
+
+import concourse.mybir as mybir
+from concourse.masks import make_identity
+
+K, H, T, S, T2, R = 1536, 1024, 2048, 512, 1024, 512
+FLOPS = 2 * 2 * K * H * S + 2 * 2 * H * T2 * R
+
+F32 = mybir.dt.float32
+BF16 = mybir.dt.bfloat16
+I32 = mybir.dt.int32
+U32 = mybir.dt.uint32
+U16 = mybir.dt.uint16
+U8 = mybir.dt.uint8
+FP8X4 = mybir.dt.float8_e4m3fn_x4
+FP4X4 = mybir.dt.float4_e2m1fn_x4
+ALU = mybir.AluOpType
+ACT = mybir.ActivationFunctionType
+
+P = 128
+KA = K // 512
+HB = H // 512
+MT = T2 // P
+
+
+def tile_list_handicap_form_book_kernel(
+    tc, tab_words, tab_scales, w1, w4_words, w4_scales, page0, wgs, low, rate, course, slot, offs, offs2, offs3, out
+):
+    nc = tc.nc
+    with ExitStack() as ctx:
+        lists = ctx.enter_context(tc.tile_pool(name="lists", bufs=1))
+        keep = ctx.enter_context(tc.tile_pool(name="keep", bufs=1))
+        psum = ctx.enter_context(tc.psum_pool(name="psum", bufs=1))
+
+        def held(shape, dtype, name, tag=None):
+            return keep.tile(shape, dtype, name=name, tag=tag or name, align_bytes=64)
+
+        banks = [psum.tile([P, 512], F32, name="bank%d" % n) for n in range(8)]
+
+        tab_sc = held([P, KA, T], U8, "tab_sc")
+        nc.vector.memset(tab_sc[:, 0:2, :].bitcast(I32), 0)
+        nc.gpsimd.memset(tab_sc[:, 2, :].bitcast(I32), 0)
+        warm = held([P, 2], F32, "warm")
+        nc.vector.memset(warm[:, 0:1], 1.0)
+        nc.scalar.activation(warm[:, 1:2], warm[:, 0:1], ACT.Abs_reciprocal_sqrt)
+        ident = held([P, P], F32, "ident")
+        make_identity(nc, ident[:])
+
+        idx = lists.tile([P, S // 16], U16, name="idx")
+        idx2 = lists.tile([P, S // 16], U16, name="idx2")
+        idx3 = lists.tile([P, R // 16], U16, name="idx3")
+
+        def load_planes(tile, src):
+            for q in range(4):
+                nc.sync.dma_start(
+                    tile[32 * q : 32 * q + 4].bitcast(I32),
+                    src[:, 4 * q : 4 * q + 4, :].rearrange("a r n -> r a n").bitcast(I32),
+                )
+
+        tab = [held([P, T], U32, "tab%d" % a, "big%d" % a) for a in range(KA)]
+        w1_raw = {(a, b): held([P, 4 * 512], F32, "w1raw%d%d" % (a, b)) for a in range(KA) for b in range(HB)}
+        w4_raw = [held([P, KA, 1024], U8, "w4raw%d" % b) for b in range(HB)]
+        w4_sc_raw = held([P, KA, H], U8, "w4_sc_raw")
+        page = [held([P, T2], F32, "page%d" % s) for s in range(8)]
+        wgs_raw = held([P, S], F32, "wgs_raw")
+
+        def load_tab(a):
+            nc.sync.dma_start(tab[a][:].bitcast(I32), tab_words[a].rearrange("p t i -> p (t i)").bitcast(I32))
+
+        def load_w1(a, b):
+            nc.sync.dma_start(
+                w1_raw[a, b][:].rearrange("p (j c) -> p j c", j=4),
+                w1[512 * a : 512 * (a + 1), 512 * b : 512 * (b + 1)].rearrange("(p j) c -> p j c", j=4),
+            )
+
+        def load_w4(b):
+            nc.sync.dma_start(
+                w4_raw[b][:].bitcast(I32),
+                w4_words[:, :, 1024 * b : 1024 * (b + 1)].rearrange("a p c -> p a c").bitcast(I32),
+            )
+
+        page_rows = page0.rearrange("(b g t i) m -> b t g i m", b=HB, g=16, t=4)
+        course_rows = course.rearrange("(b g t i) j -> b t g i j", b=HB, g=16, t=4)
+
+        def load_page(s):
+            nc.sync.dma_start(page[s][:], page_rows[s // 4, s % 4])
+
+        nc.sync.dma_start(idx[:], offs)
+        load_planes(tab_sc, tab_scales)
+        load_planes(w4_sc_raw, w4_scales)
+        load_tab(0)
+        nc.sync.dma_start(wgs_raw[:], wgs)
+        load_w1(0, 0)
+        load_w4(0)
+        nc.sync.dma_start(idx2[:], offs2)
+        nc.sync.dma_start(idx3[:], offs3)
+        load_tab(1)
+        load_w1(1, 0)
+        load_tab(2)
+        load_w1(2, 0)
+        load_w4(1)
+        for s in range(3):
+            load_page(s)
+        load_w1(0, 1)
+        load_page(3)
+        load_w1(1, 1)
+        load_w1(2, 1)
+        vec_rows = held([P, P], F32, "vec_rows")
+        for part in (slice(0, 8), slice(32, 64), slice(64, P)):
+            nc.gpsimd.memset(vec_rows[part, :], 0.0)
+        for n, vec in enumerate((low, rate)):
+            for b in range(HB):
+                first = 8 + 8 * n + 4 * b
+                nc.sync.dma_start(
+                    vec_rows[first : first + 4, :], vec.rearrange("(b g t i) -> b t g i", b=HB, g=16, t=4)[b]
+                )
+        nc.sync.dma_start(vec_rows[24:32, :], slot.rearrange("(n p) -> n p", p=P))
+        for s in range(4, 8):
+            load_page(s)
+
+        v_words = [held([P, S], U32, "vw%d" % a, tag) for a, tag in enumerate(("vw0", "w1raw00", "w1raw10"))]
+        v_sc = [held([P, S], U8, "vs%d" % a) for a in range(KA)]
+        for a in range(KA):
+            nc.vector.tensor_copy(v_sc[a][:], tab_sc[:, a, :].indirect(idx[:]))
+        w4_sc = held([P, KA, H], U8, "w4_sc")
+        nc.vector.memset(w4_sc[:].bitcast(I32), 0)
+        for q in range(4):
+            live = slice(32 * q, 32 * q + 4)
+            nc.vector.tensor_copy(
+                w4_sc[live].bitcast(I32).rearrange("p a (b t g w) -> p (a b) t g w", b=HB, t=4, g=16),
+                w4_sc_raw[live].bitcast(I32).rearrange("p a (b g t w) -> p (a b) t g w", b=HB, t=4, g=16),
+            )
+
+        w1_codes = {(a, b): held([P, 512], U32, "w1c%d%d" % (a, b)) for a in range(KA) for b in range(HB)}
+        w1_sc = {(a, b): held([P, 512], U8, "w1s%d%d" % (a, b)) for a in range(KA) for b in range(HB)}
+        w4_codes = [held([P, KA, 1024], U8, "w4c0"), held([P, KA, 1024], U8, "w4c1", "big2")]
+        stages = [held([P, 2048], BF16, "stage%d" % n) for n in range(3)]
+
+        def as_f32(tile):
+            return tile[:, 0:1024].bitcast(F32)
+
+        def deal_w4(b):
+            nc.vector.tensor_copy(
+                w4_codes[b][:].bitcast(I32).rearrange("p a (t g w) -> p a t g w", t=4, g=16),
+                w4_raw[b][:].bitcast(I32).rearrange("p a (g t w) -> p a t g w", t=4, g=16),
+            )
+
+        def quantize(codes, scales, woven):
+            nc.vector.quantize_mx(codes.bitcast(FP8X4), scales, woven)
+
+        def quant_w1(a, b, stage, fine):
+            src = w1_raw[a, b][:].rearrange("p (j g t h i) -> p t g h j i", j=4, g=16, t=4, h=2)
+            for t in range(4):
+                part = stage[:, 512 * t : 512 * (t + 1)]
+                nc.scalar.copy(part.rearrange("p (g h i j) -> p g h j i", g=16, h=2, i=4), src[:, t])
+                if fine:
+                    cols = slice(P * t, P * (t + 1))
+                    quantize(w1_codes[a, b][:, cols], w1_sc[a, b][:, cols], part)
+            if not fine:
+                quantize(w1_codes[a, b][:], w1_sc[a, b][:], stage[:])
+
+        h_own = [held([P, S], F32, "h%d" % n) for n in range(2)]
+        own_size = held([P, S], F32, "own_size")
+        spare = [w1_raw[2, 0][:, S * n : S * (n + 1)] for n in range(4)]
+        sizes = [as_f32(stages[0]), as_f32(stages[1]), own_size[:]] + spare + [spare[0]]
+        w4_bank = [0, 1, 2, 2, 2, 2, 2, 2]
+        w1_bank = [2, 3, 3, 3, 0, 1, 3, 0]
+
+        def w4_pass(s, a):
+            b, t = divmod(s, 4)
+            nc.tensor.matmul_mx(
+                banks[w4_bank[s]][:],
+                lhsT=w4_codes[b][:, a, 2 * P * t : 2 * P * (t + 1)].bitcast(FP4X4),
+                lhsT_scale=w4_sc[:, a, P * s : P * (s + 1)],
+                rhs=v_words[a][:].bitcast(FP8X4),
+                rhs_scale=v_sc[a][:],
+                start=(a == 0),
+                stop=(a == KA - 1),
+            )
+            if a == KA - 1:
+                nc.scalar.activation(sizes[s], banks[w4_bank[s]][:], ACT.Abs)
+
+        def w1_pass(s, a):
+            b, t = divmod(s, 4)
+            cols = slice(P * t, P * (t + 1))
+            nc.tensor.matmul_mx(
+                banks[w1_bank[s]][:],
+                lhsT=w1_codes[a, b][:, cols].bitcast(FP8X4),
+                lhsT_scale=w1_sc[a, b][:, cols],
+                rhs=v_words[a][:].bitcast(FP8X4),
+                rhs_scale=v_sc[a][:],
+                start=(a == 0),
+                stop=(a == KA - 1),
+            )
+
+        def products(s):
+            for a in range(KA):
+                w4_pass(s, a)
+            for a in range(KA):
+                w1_pass(s, a)
+
+        nc.vector.tensor_copy(v_words[0][:], tab[0][:].indirect(idx[:]))
+        deal_w4(0)
+        quant_w1(0, 0, stages[0], False)
+
+        wg = [held([P, S], F32, "wg%d" % t) for t in range(4)]
+        for c in range(4):
+            nc.tensor.transpose(banks[4][:, P * c : P * (c + 1)], wgs_raw[:, P * c : P * (c + 1)], ident[:])
+        by_t = banks[4][:].rearrange("p (c g t i) -> p t c g i", c=4, g=4, t=4)
+        spread = [h_own[0][:], h_own[1][:], as_f32(stages[1]), as_f32(stages[2])]
+        for t in range(4):
+            nc.scalar.copy(
+                spread[t].rearrange("p (c u g i) -> p c u g i", c=4, u=4, g=4),
+                by_t[:, t].unsqueeze(2).to_broadcast([P, 4, 4, 4, 8]),
+            )
+            back = banks[5 + t % 3]
+            for c in range(4):
+                nc.tensor.transpose(back[:, P * c : P * (c + 1)], spread[t][:, P * c : P * (c + 1)], ident[:])
+            nc.scalar.copy(wg[t][:], back[:])
+
+        nc.vector.tensor_copy(v_words[1][:], tab[1][:].indirect(idx[:]))
+        quant_w1(1, 0, stages[1], False)
+        nc.vector.tensor_copy(v_words[2][:], tab[2][:].indirect(idx[:]))
+        for a in range(KA - 1):
+            for s in range(2):
+                w4_pass(s, a)
+                w1_pass(s, a)
+        w4_pass(0, KA - 1)
+        quant_w1(2, 0, stages[2], True)
+        w1_pass(0, KA - 1)
+        w4_pass(1, KA - 1)
+        w1_pass(1, KA - 1)
+        deal_w4(1)
+
+        course_raw = [held([P, 4 * R], F32, "craw%d" % b, "big%d" % b) for b in range(HB)]
+        for b in range(HB):
+            for t in range(4):
+                nc.sync.dma_start(course_raw[b][:, R * t : R * (t + 1)], course_rows[b, t])
+
+        def weave(engine_copy, dst, src):
+            engine_copy(dst.rearrange("p (c i t) -> p c t i", i=4, t=4), src.rearrange("p t (c i) -> p c t i", i=4))
+
+        page_codes = [held([P, T2], U32, "pc%d" % b) for b in range(HB)]
+        page_sc = [held([P, T2], U8, "ps%d" % b) for b in range(HB)]
+        course_codes = [held([P, R], U32, "cc%d" % b) for b in range(HB)]
+        course_sc = [held([P, R], U8, "cs%d" % b) for b in range(HB)]
+        page_bf = [
+            raw[:].bitcast(BF16).rearrange("p (t m) -> p t m", t=4) for raw in (w1_raw[2, 1], course_raw[1])
+        ]
+
+        def revise(s, h):
+            nc.vector.tensor_tensor(h, banks[w1_bank[s]][:], sizes[s], ALU.add)
+            nc.vector.tensor_tensor(page[s][:].indirect(idx2[:]), h, wg[s % 4][:], ALU.mult)
+
+        def round_page(s):
+            nc.scalar.copy(page_bf[s // 4][:, s % 4, :], page[s][:])
+
+        def quant_course(b, stage):
+            weave(nc.scalar.copy, stage, course_raw[b][:].rearrange("p (t j) -> p t j", t=4))
+            quantize(course_codes[b][:], course_sc[b][:], stage)
+
+        halves = [held([P, 2048], BF16, "half%d" % n) for n in range(2)]
+        course_stage = [w1_raw[2, 1][:, 1024 * b : 1024 * (b + 1)].bitcast(BF16) for b in range(HB)]
+        last_h = w1_raw[2, 1][:, 1024 : 1024 + S]
+        revise(0, h_own[0][:])
+        revise(1, as_f32(stages[2]))
+        products(2)
+        quant_w1(0, 1, stages[0], False)
+        revise(2, as_f32(stages[0]))
+        products(3)
+        quant_w1(1, 1, stages[1], False)
+        quant_w1(2, 1, stages[2], False)
+        revise(3, as_f32(stages[2]))
+        products(4)
+        products(5)
+        nc.tensor.transpose(banks[3][:, 0:P], vec_rows[:], ident[:])
+        vec_cols = held([P, 32], F32, "vec_cols")
+        nc.scalar.copy(vec_cols[:], banks[3][:, 0:32])
+        products(6)
+        revise(4, h_own[0][:])
+        products(7)
+        revise(5, h_own[1][:])
+        for s in range(4):
+            round_page(s)
+        for u in range(2):
+            cols = slice(512 * u, 512 * (u + 1))
+            weave(nc.scalar.copy, halves[u][:], page_bf[0][:, :, cols])
+            quantize(page_codes[0][:, cols], page_sc[0][:, cols], halves[u][:])
+        revise(6, as_f32(halves[1]))
+        for b in range(HB):
+            quant_course(b, course_stage[b])
+        revise(7, last_h)
+        for s in range(4, 8):
+            round_page(s)
+
+        def stage_two(acc, n, codes, scales):
+            cols = slice(P * n, P * (n + 1))
+            for b in range(HB):
+                nc.tensor.matmul_mx(
+                    acc[:],
+                    lhsT=page_codes[b][:, cols].bitcast(FP8X4),
+                    lhsT_scale=page_sc[b][:, cols],
+                    rhs=codes[b][:].bitcast(FP8X4),
+                    rhs_scale=scales[b][:],
+                    start=(b == 0),
+                    stop=(b == HB - 1),
+                )
+
+        x_codes = [held([P, R], U32, "xc%d" % b) for b in range(HB)]
+        x_sc = [held([P, R], U8, "xs%d" % b) for b in range(HB)]
+        x_bf = [held([P, 4, R], BF16, "xbf%d" % b)[:] for b in range(HB)]
+        damp = [w1_raw[n // 4, 1][:, R * (n % 4) : R * (n % 4 + 1)] for n in range(MT)]
+        quarters = [held([P, 1024], BF16, "quarter%d" % c) for c in range(4)]
+        x_woven = [halves[0], stages[1]]
+        roots = [held([P, R], F32, "root%d" % n) for n in range(2)]
+
+        def pick(s, picked):
+            nc.vector.tensor_copy(picked, page[s][:].indirect(idx3[:]))
+
+        def rate_rivals(s, picked):
+            nc.vector.tensor_scalar(
+                x_bf[s // 4][:, s % 4, :], picked, vec_cols[:, 8 + s : 9 + s], vec_cols[:, 16 + s : 17 + s], ALU.max, ALU.mult
+            )
+
+        def damping(n, root):
+            acc = banks[(4 + n) % 8]
+            stage_two(acc, n, course_codes, course_sc)
+            nc.scalar.activation(spare[n % 4], acc[:], ACT.Abs)
+            nc.scalar.activation(root, spare[n % 4], ACT.Abs_reciprocal_sqrt, bias=1.0)
+            nc.scalar.activation(damp[n], root, ACT.Square)
+
+        picked = last_h
+        for c in range(4):
+            pick(c, picked)
+            cols = slice(256 * c, 256 * (c + 1))
+            weave(nc.vector.tensor_copy if c == 0 else nc.scalar.copy, quarters[c][:], page_bf[1][:, :, cols])
+            rate_rivals(c, picked)
+            quantize(page_codes[1][:, cols], page_sc[1][:, cols], quarters[c][:])
+            picked = as_f32(quarters[c])
+        damping(0, roots[0][:])
+        damping(1, roots[1][:])
+        damping(2, as_f32(x_woven[0]))
+        for s, picked in ((4, as_f32(quarters[3])), (5, as_f32(quarters[0]))):
+            pick(s, picked)
+            rate_rivals(s, picked)
+        weave(nc.scalar.copy, x_woven[0][:], x_bf[0])
+        quantize(x_codes[0][:], x_sc[0][:], x_woven[0][:])
+        for s, picked in ((6, as_f32(x_woven[0])), (7, as_f32(quarters[1]))):
+            pick(s, picked)
+            rate_rivals(s, picked)
+        damping(3, roots[0][:])
+        damping(4, x_woven[1][:, 1024:2048].bitcast(F32))
+        weave(nc.vector.tensor_copy, x_woven[1][:, 0:1024], x_bf[1][:, :, 0:256])
+        weave(nc.scalar.copy, x_woven[1][:, 1024:2048], x_bf[1][:, :, 256:R])
+        quantize(x_codes[1][:], x_sc[1][:], x_woven[1][:])
+        for n in range(5, MT):
+            damping(n, roots[n % 2][:])
+
+        results = wg + h_own + [as_f32(stages[0]), as_f32(stages[2])]
+        for n in range(MT):
+            acc = banks[(4 + n) % 8]
+            stage_two(acc, n, x_codes, x_sc)
+            res = results[n][:]
+            nc.vector.scalar_tensor_tensor(res, acc[:], vec_cols[:, 24 + n : 25 + n], damp[n], ALU.mult, ALU.mult)
+            nc.sync.dma_start(out[P * n : P * (n + 1), :], res)

@@ -38,8 +38,9 @@ def tile_list_handicap_form_book_kernel(
         banks = [psum.tile([P, 512], F32, name="bank%d" % n) for n in range(8)]
 
         tab_sc = held([P, KA, T], U8, "tab_sc")
-        nc.vector.memset(tab_sc[:, 0:2, :].bitcast(I32), 0)
-        nc.gpsimd.memset(tab_sc[:, 2, :].bitcast(I32), 0)
+        tab_sc_words = tab_sc[:].rearrange("p a n -> p (a n)").bitcast(I32)
+        nc.vector.memset(tab_sc_words[:, 0:768], 0)
+        nc.gpsimd.memset(tab_sc_words[:, 768:1536], 0)
         warm = held([P, 2], F32, "warm")
         nc.vector.memset(warm[:, 0:1], 1.0)
         nc.scalar.activation(warm[:, 1:2], warm[:, 0:1], ACT.Abs_reciprocal_sqrt)
@@ -59,7 +60,7 @@ def tile_list_handicap_form_book_kernel(
 
         tab = [held([P, T], U32, "tab%d" % a, "big%d" % a) for a in range(KA)]
         w1_raw = {(a, b): held([P, 4 * 512], F32, "w1raw%d%d" % (a, b)) for a in range(KA) for b in range(HB)}
-        w4_raw = [held([P, KA, 1024], U8, "w4raw%d" % b) for b in range(HB)]
+        w4_raw = held([P, KA, 2 * H], U8, "w4raw")
         w4_sc_raw = held([P, KA, H], U8, "w4_sc_raw")
         page = [held([P, T2], F32, "page%d" % s) for s in range(8)]
         wgs_raw = held([P, S], F32, "wgs_raw")
@@ -73,12 +74,6 @@ def tile_list_handicap_form_book_kernel(
                 w1[512 * a : 512 * (a + 1), 512 * b : 512 * (b + 1)].rearrange("(p j) c -> p j c", j=4),
             )
 
-        def load_w4(b):
-            nc.sync.dma_start(
-                w4_raw[b][:].bitcast(I32),
-                w4_words[:, :, 1024 * b : 1024 * (b + 1)].rearrange("a p c -> p a c").bitcast(I32),
-            )
-
         page_rows = page0.rearrange("(b g t i) m -> b t g i m", b=HB, g=16, t=4)
         course_rows = course.rearrange("(b g t i) j -> b t g i j", b=HB, g=16, t=4)
 
@@ -87,18 +82,16 @@ def tile_list_handicap_form_book_kernel(
 
         nc.sync.dma_start(idx[:], offs)
         load_planes(tab_sc, tab_scales)
-        load_planes(w4_sc_raw, w4_scales)
-        load_tab(0)
         nc.sync.dma_start(wgs_raw[:], wgs)
-        load_w1(0, 0)
-        load_w4(0)
-        nc.sync.dma_start(idx2[:], offs2)
-        nc.sync.dma_start(idx3[:], offs3)
+        load_tab(0)
         load_tab(1)
+        load_w1(0, 0)
+        nc.sync.dma_start(w4_raw[:].bitcast(I32), w4_words.rearrange("a p c -> p a c").bitcast(I32))
+        load_planes(w4_sc_raw, w4_scales)
         load_w1(1, 0)
         load_tab(2)
         load_w1(2, 0)
-        load_w4(1)
+        nc.sync.dma_start(idx2[:], offs2)
         for s in range(3):
             load_page(s)
         load_w1(0, 1)
@@ -117,8 +110,9 @@ def tile_list_handicap_form_book_kernel(
         nc.sync.dma_start(vec_rows[24:32, :], slot.rearrange("(n p) -> n p", p=P))
         for s in range(4, 8):
             load_page(s)
+        nc.sync.dma_start(idx3[:], offs3)
 
-        v_words = [held([P, S], U32, "vw%d" % a, tag) for a, tag in enumerate(("vw0", "w1raw00", "w1raw10"))]
+        v_words = [held([P, S], U32, "vw%d" % a, tag) for a, tag in enumerate(("vw0", "vw1", "w4raw"))]
         v_sc = [held([P, S], U8, "vs%d" % a) for a in range(KA)]
         for a in range(KA):
             nc.vector.tensor_copy(v_sc[a][:], tab_sc[:, a, :].indirect(idx[:]))
@@ -133,17 +127,11 @@ def tile_list_handicap_form_book_kernel(
 
         w1_codes = {(a, b): held([P, 512], U32, "w1c%d%d" % (a, b)) for a in range(KA) for b in range(HB)}
         w1_sc = {(a, b): held([P, 512], U8, "w1s%d%d" % (a, b)) for a in range(KA) for b in range(HB)}
-        w4_codes = [held([P, KA, 1024], U8, "w4c0"), held([P, KA, 1024], U8, "w4c1", "big2")]
+        w4_codes = held([P, KA, 2 * H], U8, "w4c")
         stages = [held([P, 2048], BF16, "stage%d" % n) for n in range(3)]
 
         def as_f32(tile):
             return tile[:, 0:1024].bitcast(F32)
-
-        def deal_w4(b):
-            nc.vector.tensor_copy(
-                w4_codes[b][:].bitcast(I32).rearrange("p a (t g w) -> p a t g w", t=4, g=16),
-                w4_raw[b][:].bitcast(I32).rearrange("p a (g t w) -> p a t g w", t=4, g=16),
-            )
 
         def quantize(codes, scales, woven):
             nc.vector.quantize_mx(codes.bitcast(FP8X4), scales, woven)
@@ -152,25 +140,25 @@ def tile_list_handicap_form_book_kernel(
             src = w1_raw[a, b][:].rearrange("p (j g t h i) -> p t g h j i", j=4, g=16, t=4, h=2)
             for t in range(4):
                 part = stage[:, 512 * t : 512 * (t + 1)]
-                nc.scalar.copy(part.rearrange("p (g h i j) -> p g h j i", g=16, h=2, i=4), src[:, t])
+                engine_copy = nc.vector.tensor_copy if fine else nc.scalar.copy
+                engine_copy(part.rearrange("p (g h i j) -> p g h j i", g=16, h=2, i=4), src[:, t])
                 if fine:
                     cols = slice(P * t, P * (t + 1))
                     quantize(w1_codes[a, b][:, cols], w1_sc[a, b][:, cols], part)
             if not fine:
                 quantize(w1_codes[a, b][:], w1_sc[a, b][:], stage[:])
 
-        h_own = [held([P, S], F32, "h%d" % n) for n in range(2)]
-        own_size = held([P, S], F32, "own_size")
-        spare = [w1_raw[2, 0][:, S * n : S * (n + 1)] for n in range(4)]
-        sizes = [as_f32(stages[0]), as_f32(stages[1]), own_size[:]] + spare + [spare[0]]
+        h_own = [held([P, S], F32, "h%d" % n) for n in range(3)]
+        spare = [stages[n // 2][:, 1024 * (n % 2) : 1024 * (n % 2 + 1)].bitcast(F32) for n in range(4)]
+        sizes = [h_own[2][:], spare[0], as_f32(stages[2]), spare[1]]
+        sizes = sizes + [w1_raw[2, 1][:, 3 * S : 4 * S], spare[3], spare[0], spare[1]]
         w4_bank = [0, 1, 2, 2, 2, 2, 2, 2]
-        w1_bank = [2, 3, 3, 3, 0, 1, 3, 0]
+        w1_bank = [2, 3, 3, 3, 0, 1, 4, 5]
 
         def w4_pass(s, a):
-            b, t = divmod(s, 4)
             nc.tensor.matmul_mx(
                 banks[w4_bank[s]][:],
-                lhsT=w4_codes[b][:, a, 2 * P * t : 2 * P * (t + 1)].bitcast(FP4X4),
+                lhsT=w4_codes[:, a, 2 * P * s : 2 * P * (s + 1)].bitcast(FP4X4),
                 lhsT_scale=w4_sc[:, a, P * s : P * (s + 1)],
                 rhs=v_words[a][:].bitcast(FP8X4),
                 rhs_scale=v_sc[a][:],
@@ -199,15 +187,11 @@ def tile_list_handicap_form_book_kernel(
             for a in range(KA):
                 w1_pass(s, a)
 
-        nc.vector.tensor_copy(v_words[0][:], tab[0][:].indirect(idx[:]))
-        deal_w4(0)
-        quant_w1(0, 0, stages[0], False)
-
         wg = [held([P, S], F32, "wg%d" % t) for t in range(4)]
         for c in range(4):
             nc.tensor.transpose(banks[4][:, P * c : P * (c + 1)], wgs_raw[:, P * c : P * (c + 1)], ident[:])
         by_t = banks[4][:].rearrange("p (c g t i) -> p t c g i", c=4, g=4, t=4)
-        spread = [h_own[0][:], h_own[1][:], as_f32(stages[1]), as_f32(stages[2])]
+        spread = [h_own[0][:], h_own[1][:], h_own[2][:], as_f32(stages[1])]
         for t in range(4):
             nc.scalar.copy(
                 spread[t].rearrange("p (c u g i) -> p c u g i", c=4, u=4, g=4),
@@ -218,6 +202,13 @@ def tile_list_handicap_form_book_kernel(
                 nc.tensor.transpose(back[:, P * c : P * (c + 1)], spread[t][:, P * c : P * (c + 1)], ident[:])
             nc.scalar.copy(wg[t][:], back[:])
 
+        nc.vector.tensor_copy(v_words[0][:], tab[0][:].indirect(idx[:]))
+        nc.vector.tensor_copy(
+            w4_codes[:].bitcast(I32).rearrange("p a (b t g w) -> p (a b) t g w", b=HB, t=4, g=16),
+            w4_raw[:].bitcast(I32).rearrange("p a (b g t w) -> p (a b) t g w", b=HB, t=4, g=16),
+        )
+        quant_w1(0, 0, stages[0], False)
+
         nc.vector.tensor_copy(v_words[1][:], tab[1][:].indirect(idx[:]))
         quant_w1(1, 0, stages[1], False)
         nc.vector.tensor_copy(v_words[2][:], tab[2][:].indirect(idx[:]))
@@ -226,11 +217,10 @@ def tile_list_handicap_form_book_kernel(
                 w4_pass(s, a)
                 w1_pass(s, a)
         w4_pass(0, KA - 1)
-        quant_w1(2, 0, stages[2], True)
+        quant_w1(2, 0, stages[1], True)
         w1_pass(0, KA - 1)
         w4_pass(1, KA - 1)
         w1_pass(1, KA - 1)
-        deal_w4(1)
 
         course_raw = [held([P, 4 * R], F32, "craw%d" % b, "big%d" % b) for b in range(HB)]
         for b in range(HB):
@@ -248,9 +238,15 @@ def tile_list_handicap_form_book_kernel(
             raw[:].bitcast(BF16).rearrange("p (t m) -> p t m", t=4) for raw in (w1_raw[2, 1], course_raw[1])
         ]
 
-        def revise(s, h):
-            nc.vector.tensor_tensor(h, banks[w1_bank[s]][:], sizes[s], ALU.add)
-            nc.vector.tensor_tensor(page[s][:].indirect(idx2[:]), h, wg[s % 4][:], ALU.mult)
+        features = [h_own[1][:], stages[2][:, 1024:2048].bitcast(F32), h_own[0][:]]
+        features = features + [as_f32(stages[2])]
+        features = features + [features[3], h_own[2][:], h_own[0][:], w1_raw[2, 1][:, 0:S]]
+
+        def add_up(s):
+            nc.vector.tensor_tensor(features[s], banks[w1_bank[s]][:], sizes[s], ALU.add)
+
+        def put(s):
+            nc.vector.tensor_tensor(page[s][:].indirect(idx2[:]), features[s], wg[s % 4][:], ALU.mult)
 
         def round_page(s):
             nc.scalar.copy(page_bf[s // 4][:, s % 4, :], page[s][:])
@@ -261,35 +257,42 @@ def tile_list_handicap_form_book_kernel(
 
         halves = [held([P, 2048], BF16, "half%d" % n) for n in range(2)]
         course_stage = [w1_raw[2, 1][:, 1024 * b : 1024 * (b + 1)].bitcast(BF16) for b in range(HB)]
-        last_h = w1_raw[2, 1][:, 1024 : 1024 + S]
-        revise(0, h_own[0][:])
-        revise(1, as_f32(stages[2]))
+        add_up(0)
+        put(0)
+        add_up(1)
+        put(1)
         products(2)
-        quant_w1(0, 1, stages[0], False)
-        revise(2, as_f32(stages[0]))
+        add_up(2)
+        put(2)
         products(3)
-        quant_w1(1, 1, stages[1], False)
+        for a in range(2):
+            quant_w1(a, 1, w1_raw[2, 0][:, 1024 * a : 1024 * (a + 1)].bitcast(BF16), False)
         quant_w1(2, 1, stages[2], False)
-        revise(3, as_f32(stages[2]))
+        add_up(3)
+        put(3)
         products(4)
         products(5)
         nc.tensor.transpose(banks[3][:, 0:P], vec_rows[:], ident[:])
         vec_cols = held([P, 32], F32, "vec_cols")
         nc.scalar.copy(vec_cols[:], banks[3][:, 0:32])
         products(6)
-        revise(4, h_own[0][:])
+        add_up(4)
         products(7)
-        revise(5, h_own[1][:])
+        add_up(5)
+        put(4)
+        add_up(6)
+        put(5)
+        put(6)
         for s in range(4):
             round_page(s)
         for u in range(2):
             cols = slice(512 * u, 512 * (u + 1))
             weave(nc.scalar.copy, halves[u][:], page_bf[0][:, :, cols])
             quantize(page_codes[0][:, cols], page_sc[0][:, cols], halves[u][:])
-        revise(6, as_f32(halves[1]))
-        for b in range(HB):
-            quant_course(b, course_stage[b])
-        revise(7, last_h)
+        quant_course(0, course_stage[0])
+        add_up(7)
+        quant_course(1, course_stage[1])
+        put(7)
         for s in range(4, 8):
             round_page(s)
 
@@ -308,10 +311,12 @@ def tile_list_handicap_form_book_kernel(
 
         x_codes = [held([P, R], U32, "xc%d" % b) for b in range(HB)]
         x_sc = [held([P, R], U8, "xs%d" % b) for b in range(HB)]
-        x_bf = [held([P, 4, R], BF16, "xbf%d" % b)[:] for b in range(HB)]
+        x_space = held([P, 3 * 1024], BF16, "x_space")
+        x_flat = [halves[0][:], x_space[:, 0:2048]]
+        x_bf = [flat.rearrange("p (t j) -> p t j", t=4) for flat in x_flat]
         damp = [w1_raw[n // 4, 1][:, R * (n % 4) : R * (n % 4 + 1)] for n in range(MT)]
         quarters = [held([P, 1024], BF16, "quarter%d" % c) for c in range(4)]
-        x_woven = [halves[0], stages[1]]
+        x_woven = [x_space[:, 1024:3072], halves[1][:]]
         roots = [held([P, R], F32, "root%d" % n) for n in range(2)]
 
         def pick(s, picked):
@@ -322,41 +327,46 @@ def tile_list_handicap_form_book_kernel(
                 x_bf[s // 4][:, s % 4, :], picked, vec_cols[:, 8 + s : 9 + s], vec_cols[:, 16 + s : 17 + s], ALU.max, ALU.mult
             )
 
-        def damping(n, root):
+        def damping(n, size, root):
             acc = banks[(4 + n) % 8]
             stage_two(acc, n, course_codes, course_sc)
-            nc.scalar.activation(spare[n % 4], acc[:], ACT.Abs)
-            nc.scalar.activation(root, spare[n % 4], ACT.Abs_reciprocal_sqrt, bias=1.0)
+            nc.scalar.activation(size, acc[:], ACT.Abs)
+            nc.scalar.activation(root, size, ACT.Abs_reciprocal_sqrt, bias=1.0)
             nc.scalar.activation(damp[n], root, ACT.Square)
 
-        picked = last_h
+        picked = [features[7]] + [as_f32(quarter) for quarter in quarters]
+        picked = picked + picked[1:4]
         for c in range(4):
-            pick(c, picked)
+            pick(c, picked[c])
             cols = slice(256 * c, 256 * (c + 1))
             weave(nc.vector.tensor_copy if c == 0 else nc.scalar.copy, quarters[c][:], page_bf[1][:, :, cols])
-            rate_rivals(c, picked)
+            if c == 0:
+                rate_rivals(c, picked[c])
             quantize(page_codes[1][:, cols], page_sc[1][:, cols], quarters[c][:])
-            picked = as_f32(quarters[c])
-        damping(0, roots[0][:])
-        damping(1, roots[1][:])
-        damping(2, as_f32(x_woven[0]))
-        for s, picked in ((4, as_f32(quarters[3])), (5, as_f32(quarters[0]))):
-            pick(s, picked)
-            rate_rivals(s, picked)
-        weave(nc.scalar.copy, x_woven[0][:], x_bf[0])
-        quantize(x_codes[0][:], x_sc[0][:], x_woven[0][:])
-        for s, picked in ((6, as_f32(x_woven[0])), (7, as_f32(quarters[1]))):
-            pick(s, picked)
-            rate_rivals(s, picked)
-        damping(3, roots[0][:])
-        damping(4, x_woven[1][:, 1024:2048].bitcast(F32))
+            if c > 0:
+                rate_rivals(c, picked[c])
+        for s in range(4, 8):
+            pick(s, picked[s])
+        for s in (4, 5):
+            rate_rivals(s, picked[s])
+        damping(0, spare[0], roots[0][:])
+        damping(1, spare[1], roots[1][:])
+        damping(2, spare[2], as_f32(x_woven[0]))
+        weave(nc.scalar.copy, x_woven[0], x_bf[0])
+        quantize(x_codes[0][:], x_sc[0][:], x_woven[0])
+        for s in (6, 7):
+            rate_rivals(s, picked[s])
+        damping(3, spare[3], roots[0][:])
+        damping(4, spare[0], x_woven[1][:, 1024:2048].bitcast(F32))
         weave(nc.vector.tensor_copy, x_woven[1][:, 0:1024], x_bf[1][:, :, 0:256])
         weave(nc.scalar.copy, x_woven[1][:, 1024:2048], x_bf[1][:, :, 256:R])
-        quantize(x_codes[1][:], x_sc[1][:], x_woven[1][:])
+        for cols in (slice(0, 256), slice(256, R)):
+            quantize(x_codes[1][:, cols], x_sc[1][:, cols], x_woven[1][:, 4 * cols.start : 4 * cols.stop])
         for n in range(5, MT):
-            damping(n, roots[n % 2][:])
+            late = x_flat[1][:, 1024 * (n % 2) : 1024 * (n % 2 + 1)].bitcast(F32)
+            damping(n, late, roots[n % 2][:])
 
-        results = wg + h_own + [as_f32(stages[0]), as_f32(stages[2])]
+        results = wg + h_own + [as_f32(stages[2])]
         for n in range(MT):
             acc = banks[(4 + n) % 8]
             stage_two(acc, n, x_codes, x_sc)

@@ -52,11 +52,8 @@ def tile_list_handicap_form_book_kernel(
         idx3 = lists.tile([P, R // 16], U16, name="idx3")
 
         def load_planes(tile, src):
-            for q in range(4):
-                nc.sync.dma_start(
-                    tile[32 * q : 32 * q + 4].bitcast(I32),
-                    src[:, 4 * q : 4 * q + 4, :].rearrange("a r n -> r a n").bitcast(I32),
-                )
+            for r in range(4):
+                nc.sync.dma_start(tile[r:P:32].bitcast(I32), src[:, r:16:4, :].rearrange("a q n -> q a n").bitcast(I32))
 
         tab = [held([P, T], U32, "tab%d" % a, "big%d" % a) for a in range(KA)]
         w1_raw = {(a, b): held([P, 4 * 512], F32, "w1raw%d%d" % (a, b)) for a in range(KA) for b in range(HB)}
@@ -92,12 +89,13 @@ def tile_list_handicap_form_book_kernel(
         load_tab(2)
         load_w1(2, 0)
         nc.sync.dma_start(idx2[:], offs2)
-        for s in range(3):
-            load_page(s)
+        load_page(0)
+        load_page(1)
         load_w1(0, 1)
-        load_page(3)
+        load_page(2)
         load_w1(1, 1)
         load_w1(2, 1)
+        load_page(3)
         vec_rows = held([P, P], F32, "vec_rows")
         for part in (slice(0, 8), slice(32, 64), slice(64, P)):
             nc.gpsimd.memset(vec_rows[part, :], 0.0)
@@ -327,12 +325,21 @@ def tile_list_handicap_form_book_kernel(
                 x_bf[s // 4][:, s % 4, :], picked, vec_cols[:, 8 + s : 9 + s], vec_cols[:, 16 + s : 17 + s], ALU.max, ALU.mult
             )
 
-        def damping(n, size, root):
+        def damp_size(n, size):
             acc = banks[(4 + n) % 8]
             stage_two(acc, n, course_codes, course_sc)
             nc.scalar.activation(size, acc[:], ACT.Abs)
+
+        def damp_root(size, root):
             nc.scalar.activation(root, size, ACT.Abs_reciprocal_sqrt, bias=1.0)
+
+        def damp_square(n, root):
             nc.scalar.activation(damp[n], root, ACT.Square)
+
+        def damping(n, size, root):
+            damp_size(n, size)
+            damp_root(size, root)
+            damp_square(n, root)
 
         picked = [features[7]] + [as_f32(quarter) for quarter in quarters]
         picked = picked + picked[1:4]
@@ -362,9 +369,14 @@ def tile_list_handicap_form_book_kernel(
         weave(nc.scalar.copy, x_woven[1][:, 1024:2048], x_bf[1][:, :, 256:R])
         for cols in (slice(0, 256), slice(256, R)):
             quantize(x_codes[1][:, cols], x_sc[1][:, cols], x_woven[1][:, 4 * cols.start : 4 * cols.stop])
-        for n in range(5, MT):
-            late = x_flat[1][:, 1024 * (n % 2) : 1024 * (n % 2 + 1)].bitcast(F32)
-            damping(n, late, roots[n % 2][:])
+        late = [x_flat[1][:, 1024 * u : 1024 * (u + 1)].bitcast(F32) for u in range(2)]
+        for step in range(5, MT + 2):
+            if step - 2 >= 5:
+                damp_square(step - 2, roots[step % 2][:])
+            if 5 <= step - 1 < MT:
+                damp_root(late[(step - 1) % 2], roots[(step - 1) % 2][:])
+            if step < MT:
+                damp_size(step, late[step % 2])
 
         results = wg + h_own + [as_f32(stages[2])]
         for n in range(MT):

@@ -37,13 +37,23 @@ def tile_list_handicap_form_book_kernel(
 
         banks = [psum.tile([P, 512], F32, name="bank%d" % n) for n in range(8)]
 
-        tab_sc = held([P, KA, T], U8, "tab_sc")
-        tab_sc_words = tab_sc[:].rearrange("p a n -> p (a n)").bitcast(I32)
-        nc.vector.memset(tab_sc_words[:, 0:768], 0)
-        nc.gpsimd.memset(tab_sc_words[:, 768:1536], 0)
+        tab_sc = held([P, T], U8, "tab_sc")
+        w4_sc_raw = held([P, H], U8, "w4_sc_raw")
+        v_sc = held([P, KA, S], U8, "v_sc")
+        w4_sc = held([P, KA, H], U8, "w4_sc")
+
+        def load_scale_rows(queue, rows, src):
+            queue.dma_start(rows[16:64, :].bitcast(I32), src.rearrange("a q n -> q a n").bitcast(I32))
+
+        load_scale_rows(nc.scalar, w4_sc_raw, w4_scales)
         warm = held([P, 2], F32, "warm")
         nc.vector.memset(warm[:, 0:1], 1.0)
         nc.scalar.activation(warm[:, 1:2], warm[:, 0:1], ACT.Abs_reciprocal_sqrt)
+        for rows in (tab_sc, w4_sc_raw):
+            nc.vector.memset(rows[0:16, :].bitcast(I32), 0)
+            nc.vector.memset(rows[64:P, :].bitcast(I32), 0)
+        nc.vector.memset(v_sc[:].bitcast(I32), 0)
+        nc.vector.memset(w4_sc[:].bitcast(I32), 0)
         ident = held([P, P], F32, "ident")
         make_identity(nc, ident[:])
 
@@ -51,14 +61,15 @@ def tile_list_handicap_form_book_kernel(
         idx2 = lists.tile([P, S // 16], U16, name="idx2")
         idx3 = lists.tile([P, R // 16], U16, name="idx3")
 
-        def load_planes(tile, src):
-            for r in range(4):
-                nc.sync.dma_start(tile[r:P:32].bitcast(I32), src[:, r:16:4, :].rearrange("a q n -> q a n").bitcast(I32))
+        def to_planes(planes, rows):
+            for q in range(4):
+                nc.gpsimd.dma_start(
+                    planes[32 * q : 32 * q + 4].bitcast(I32), rows[16 + 12 * q : 28 + 12 * q, :].bitcast(I32)
+                )
 
         tab = [held([P, T], U32, "tab%d" % a, "big%d" % a) for a in range(KA)]
         w1_raw = {(a, b): held([P, 4 * 512], F32, "w1raw%d%d" % (a, b)) for a in range(KA) for b in range(HB)}
         w4_raw = held([P, KA, 2 * H], U8, "w4raw")
-        w4_sc_raw = held([P, KA, H], U8, "w4_sc_raw")
         page = [held([P, T2], F32, "page%d" % s) for s in range(8)]
         wgs_raw = held([P, S], F32, "wgs_raw")
 
@@ -78,13 +89,12 @@ def tile_list_handicap_form_book_kernel(
             nc.sync.dma_start(page[s][:], page_rows[s // 4, s % 4])
 
         nc.sync.dma_start(idx[:], offs)
-        load_planes(tab_sc, tab_scales)
+        load_scale_rows(nc.sync, tab_sc, tab_scales)
         nc.sync.dma_start(wgs_raw[:], wgs)
         load_tab(0)
         load_tab(1)
         load_w1(0, 0)
         nc.sync.dma_start(w4_raw[:].bitcast(I32), w4_words.rearrange("a p c -> p a c").bitcast(I32))
-        load_planes(w4_sc_raw, w4_scales)
         load_w1(1, 0)
         load_tab(2)
         load_w1(2, 0)
@@ -111,17 +121,15 @@ def tile_list_handicap_form_book_kernel(
         nc.sync.dma_start(idx3[:], offs3)
 
         v_words = [held([P, S], U32, "vw%d" % a, tag) for a, tag in enumerate(("vw0", "vw1", "w4raw"))]
-        v_sc = [held([P, S], U8, "vs%d" % a) for a in range(KA)]
-        for a in range(KA):
-            nc.vector.tensor_copy(v_sc[a][:], tab_sc[:, a, :].indirect(idx[:]))
-        w4_sc = held([P, KA, H], U8, "w4_sc")
-        nc.vector.memset(w4_sc[:].bitcast(I32), 0)
-        for q in range(4):
-            live = slice(32 * q, 32 * q + 4)
-            nc.vector.tensor_copy(
-                w4_sc[live].bitcast(I32).rearrange("p a (b t g w) -> p (a b) t g w", b=HB, t=4, g=16),
-                w4_sc_raw[live].bitcast(I32).rearrange("p a (b g t w) -> p (a b) t g w", b=HB, t=4, g=16),
-            )
+        w4_sc_rows = held([P, H], U8, "w4_sc_rows")
+        nc.vector.tensor_copy(
+            w4_sc_rows[:].bitcast(I32).rearrange("p (b t g w) -> p b t g w", b=HB, t=4, g=16),
+            w4_sc_raw[:].bitcast(I32).rearrange("p (b g t w) -> p b t g w", b=HB, t=4, g=16),
+        )
+        to_planes(w4_sc, w4_sc_rows)
+        v_sc_rows = held([P, S], U8, "v_sc_rows")
+        nc.vector.tensor_copy(v_sc_rows[:], tab_sc[:].indirect(idx[:]))
+        to_planes(v_sc, v_sc_rows)
 
         w1_codes = {(a, b): held([P, 512], U32, "w1c%d%d" % (a, b)) for a in range(KA) for b in range(HB)}
         w1_sc = {(a, b): held([P, 512], U8, "w1s%d%d" % (a, b)) for a in range(KA) for b in range(HB)}
@@ -148,8 +156,14 @@ def tile_list_handicap_form_book_kernel(
 
         h_own = [held([P, S], F32, "h%d" % n) for n in range(3)]
         spare = [stages[n // 2][:, 1024 * (n % 2) : 1024 * (n % 2 + 1)].bitcast(F32) for n in range(4)]
-        sizes = [h_own[2][:], spare[0], as_f32(stages[2]), spare[1]]
+        late_stages = [held([P, 2048], BF16, "late_stage%d" % a) for a in range(2)]
+
+        def in_four(ap):
+            return ap.rearrange("p (u c) -> p u c", u=4)
+
+        sizes = [as_f32(stages[2]), spare[1]]
         sizes = sizes + [w1_raw[2, 1][:, 3 * S : 4 * S], spare[3], spare[0], spare[1]]
+        sizes = [in_four(stage[:].bitcast(F32))[:, :, 0:P] for stage in late_stages] + [in_four(ap) for ap in sizes]
         w4_bank = [0, 1, 2, 2, 2, 2, 2, 2]
         w1_bank = [2, 3, 3, 3, 0, 1, 4, 5]
 
@@ -159,12 +173,12 @@ def tile_list_handicap_form_book_kernel(
                 lhsT=w4_codes[:, a, 2 * P * s : 2 * P * (s + 1)].bitcast(FP4X4),
                 lhsT_scale=w4_sc[:, a, P * s : P * (s + 1)],
                 rhs=v_words[a][:].bitcast(FP8X4),
-                rhs_scale=v_sc[a][:],
+                rhs_scale=v_sc[:, a, :],
                 start=(a == 0),
                 stop=(a == KA - 1),
             )
             if a == KA - 1:
-                nc.scalar.activation(sizes[s], banks[w4_bank[s]][:], ACT.Abs)
+                nc.scalar.activation(sizes[s], in_four(banks[w4_bank[s]][:]), ACT.Abs)
 
         def w1_pass(s, a):
             b, t = divmod(s, 4)
@@ -174,7 +188,7 @@ def tile_list_handicap_form_book_kernel(
                 lhsT=w1_codes[a, b][:, cols].bitcast(FP8X4),
                 lhsT_scale=w1_sc[a, b][:, cols],
                 rhs=v_words[a][:].bitcast(FP8X4),
-                rhs_scale=v_sc[a][:],
+                rhs_scale=v_sc[:, a, :],
                 start=(a == 0),
                 stop=(a == KA - 1),
             )
@@ -241,7 +255,7 @@ def tile_list_handicap_form_book_kernel(
         features = features + [features[3], h_own[2][:], h_own[0][:], w1_raw[2, 1][:, 0:S]]
 
         def add_up(s):
-            nc.vector.tensor_tensor(features[s], banks[w1_bank[s]][:], sizes[s], ALU.add)
+            nc.vector.tensor_tensor(in_four(features[s]), in_four(banks[w1_bank[s]][:]), sizes[s], ALU.add)
 
         def put(s):
             nc.vector.tensor_tensor(page[s][:].indirect(idx2[:]), features[s], wg[s % 4][:], ALU.mult)
@@ -264,7 +278,7 @@ def tile_list_handicap_form_book_kernel(
         put(2)
         products(3)
         for a in range(2):
-            quant_w1(a, 1, w1_raw[2, 0][:, 1024 * a : 1024 * (a + 1)].bitcast(BF16), False)
+            quant_w1(a, 1, late_stages[a], False)
         quant_w1(2, 1, stages[2], False)
         add_up(3)
         put(3)

from contextlib import ExitStack

import concourse.mybir as mybir
from concourse.masks import make_identity

K, H, T, S, T2, R = 1536, 1024, 2048, 512, 1024, 512
FLOPS = 2 * 2 * K * H * S + 2 * 2 * H * T2 * R

F32 = mybir.dt.float32
BF16 = mybir.dt.bfloat16
I32 = mybir.dt.int32
U32 = mybir.dt.uint32
U16 = mybir.dt.uint16
U8 = mybir.dt.uint8
FP8X4 = mybir.dt.float8_e4m3fn_x4
FP4X4 = mybir.dt.float4_e2m1fn_x4
ALU = mybir.AluOpType
ACT = mybir.ActivationFunctionType

P = 128
KA = K // 512
HB = H // 512
MT = T2 // P


def tile_list_handicap_form_book_kernel(
    tc, tab_words, tab_scales, w1, w4_words, w4_scales, page0, wgs, low, rate, course, slot, offs, offs2, offs3, out
):
    nc = tc.nc
    with ExitStack() as ctx:
        lists = ctx.enter_context(tc.tile_pool(name="lists", bufs=1))
        keep = ctx.enter_context(tc.tile_pool(name="keep", bufs=1))
        psum = ctx.enter_context(tc.psum_pool(name="psum", bufs=1))

        def held(shape, dtype, name, tag=None):
            return keep.tile(shape, dtype, name=name, tag=tag or name, align_bytes=64)

        banks = [psum.tile([P, 512], F32, name="bank%d" % n) for n in range(8)]

        tab_sc = held([P, T], U8, "tab_sc")
        w4_sc_raw = held([P, H], U8, "w4_sc_raw")
        v_sc = held([P, KA, S], U8, "v_sc")
        w4_sc = held([P, KA, H], U8, "w4_sc")

        def load_scale_rows(queue, rows, src):
            queue.dma_start(rows[16:64, :].bitcast(I32), src.rearrange("a q n -> q a n").bitcast(I32))

        load_scale_rows(nc.scalar, w4_sc_raw, w4_scales)
        warm = held([P, 2], F32, "warm")
        nc.vector.memset(warm[:, 0:1], 1.0)
        nc.scalar.activation(warm[:, 1:2], warm[:, 0:1], ACT.Abs_reciprocal_sqrt)
        for rows in (tab_sc, w4_sc_raw):
            nc.vector.memset(rows[0:16, :].bitcast(I32), 0)
            nc.vector.memset(rows[64:P, :].bitcast(I32), 0)
        nc.vector.memset(v_sc[:].bitcast(I32), 0)
        nc.vector.memset(w4_sc[:].bitcast(I32), 0)
        ident = held([P, P], F32, "ident")
        make_identity(nc, ident[:])

        idx = lists.tile([P, S // 16], U16, name="idx")
        idx2 = lists.tile([P, S // 16], U16, name="idx2")
        idx3 = lists.tile([P, R // 16], U16, name="idx3")

        def to_planes(planes, rows):
            for q in range(4):
                nc.gpsimd.dma_start(
                    planes[32 * q : 32 * q + 4].bitcast(I32), rows[16 + 12 * q : 28 + 12 * q, :].bitcast(I32)
                )

        tab = [held([P, T], U32, "tab%d" % a, "big%d" % a) for a in range(KA)]
        w1_raw = {(a, b): held([P, 4 * 512], F32, "w1raw%d%d" % (a, b)) for a in range(KA) for b in range(HB)}
        w4_raw = held([P, KA, 2 * H], U8, "w4raw")
        page = [held([P, T2], F32, "page%d" % s) for s in range(8)]
        wgs_raw = held([P, S], F32, "wgs_raw")

        def load_tab(a):
            nc.sync.dma_start(tab[a][:].bitcast(I32), tab_words[a].rearrange("p t i -> p (t i)").bitcast(I32))

        def load_w1(a, b):
            nc.sync.dma_start(
                w1_raw[a, b][:].rearrange("p (j c) -> p j c", j=4),
                w1[512 * a : 512 * (a + 1), 512 * b : 512 * (b + 1)].rearrange("(p j) c -> p j c", j=4),
            )

        page_rows = page0.rearrange("(b g t i) m -> b t g i m", b=HB, g=16, t=4)
        course_rows = course.rearrange("(b g t i) j -> b t g i j", b=HB, g=16, t=4)

        def load_page(s):
            nc.sync.dma_start(page[s][:], page_rows[s // 4, s % 4])

        nc.sync.dma_start(idx[:], offs)
        load_scale_rows(nc.sync, tab_sc, tab_scales)
        nc.sync.dma_start(wgs_raw[:], wgs)
        load_tab(0)
        load_tab(1)
        load_w1(0, 0)
        nc.sync.dma_start(w4_raw[:].bitcast(I32), w4_words.rearrange("a p c -> p a c").bitcast(I32))
        load_w1(1, 0)
        load_tab(2)
        load_w1(2, 0)
        nc.sync.dma_start(idx2[:], offs2)
        load_page(0)
        load_page(1)
        load_w1(0, 1)
        load_page(2)
        load_w1(1, 1)
        load_w1(2, 1)
        load_page(3)
        vec_rows = held([P, P], F32, "vec_rows")
        for part in (slice(0, 8), slice(32, 64), slice(64, P)):
            nc.gpsimd.memset(vec_rows[part, :], 0.0)
        for n, vec in enumerate((low, rate)):
            for b in range(HB):
                first = 8 + 8 * n + 4 * b
                nc.sync.dma_start(
                    vec_rows[first : first + 4, :], vec.rearrange("(b g t i) -> b t g i", b=HB, g=16, t=4)[b]
                )
        nc.sync.dma_start(vec_rows[24:32, :], slot.rearrange("(n p) -> n p", p=P))
        for s in range(4, 8):
            load_page(s)
        nc.sync.dma_start(idx3[:], offs3)

        v_words = [held([P, S], U32, "vw%d" % a, tag) for a, tag in enumerate(("vw0", "vw1", "w4raw"))]
        w4_sc_rows = held([P, H], U8, "w4_sc_rows")
        nc.vector.tensor_copy(
            w4_sc_rows[:].bitcast(I32).rearrange("p (b t g w) -> p b t g w", b=HB, t=4, g=16),
            w4_sc_raw[:].bitcast(I32).rearrange("p (b g t w) -> p b t g w", b=HB, t=4, g=16),
        )
        to_planes(w4_sc, w4_sc_rows)
        v_sc_rows = held([P, S], U8, "v_sc_rows")
        nc.vector.tensor_copy(v_sc_rows[:], tab_sc[:].indirect(idx[:]))
        to_planes(v_sc, v_sc_rows)

        w1_codes = {(a, b): held([P, 512], U32, "w1c%d%d" % (a, b)) for a in range(KA) for b in range(HB)}
        w1_sc = {(a, b): held([P, 512], U8, "w1s%d%d" % (a, b)) for a in range(KA) for b in range(HB)}
        w4_codes = held([P, KA, 2 * H], U8, "w4c")
        stages = [held([P, 2048], BF16, "stage%d" % n) for n in range(3)]

        def as_f32(tile):
            return tile[:, 0:1024].bitcast(F32)

        def quantize(codes, scales, woven):
            nc.vector.quantize_mx(codes.bitcast(FP8X4), scales, woven)

        def quant_w1(a, b, stage, fine):
            src = w1_raw[a, b][:].rearrange("p (j g t h i) -> p t g h j i", j=4, g=16, t=4, h=2)
            for t in range(4):
                part = stage[:, 512 * t : 512 * (t + 1)]
                engine_copy = nc.vector.tensor_copy if fine else nc.scalar.copy
                engine_copy(part.rearrange("p (g h i j) -> p g h j i", g=16, h=2, i=4), src[:, t])
                if fine:
                    cols = slice(P * t, P * (t + 1))
                    quantize(w1_codes[a, b][:, cols], w1_sc[a, b][:, cols], part)
            if not fine:
                quantize(w1_codes[a, b][:], w1_sc[a, b][:], stage[:])

        h_own = [held([P, S], F32, "h%d" % n) for n in range(3)]
        spare = [stages[n // 2][:, 1024 * (n % 2) : 1024 * (n % 2 + 1)].bitcast(F32) for n in range(4)]
        late_stages = [held([P, 2048], BF16, "late_stage%d" % a) for a in range(2)]

        def in_four(ap):
            return ap.rearrange("p (u c) -> p u c", u=4)

        sizes = [as_f32(stages[2]), spare[1]]
        sizes = sizes + [w1_raw[2, 1][:, 3 * S : 4 * S], spare[3], spare[0], spare[1]]
        sizes = [in_four(stage[:].bitcast(F32))[:, :, 0:P] for stage in late_stages] + [in_four(ap) for ap in sizes]
        w4_bank = [0, 1, 2, 2, 2, 2, 2, 2]
        w1_bank = [2, 3, 3, 3, 0, 1, 4, 5]

        def w4_pass(s, a):
            nc.tensor.matmul_mx(
                banks[w4_bank[s]][:],
                lhsT=w4_codes[:, a, 2 * P * s : 2 * P * (s + 1)].bitcast(FP4X4),
                lhsT_scale=w4_sc[:, a, P * s : P * (s + 1)],
                rhs=v_words[a][:].bitcast(FP8X4),
                rhs_scale=v_sc[:, a, :],
                start=(a == 0),
                stop=(a == KA - 1),
            )
            if a == KA - 1:
                nc.scalar.activation(sizes[s], in_four(banks[w4_bank[s]][:]), ACT.Abs)

        def w1_pass(s, a):
            b, t = divmod(s, 4)
            cols = slice(P * t, P * (t + 1))
            nc.tensor.matmul_mx(
                banks[w1_bank[s]][:],
                lhsT=w1_codes[a, b][:, cols].bitcast(FP8X4),
                lhsT_scale=w1_sc[a, b][:, cols],
                rhs=v_words[a][:].bitcast(FP8X4),
                rhs_scale=v_sc[:, a, :],
                start=(a == 0),
                stop=(a == KA - 1),
            )

        def products(s):
            for a in range(KA):
                w4_pass(s, a)
            for a in range(KA):
                w1_pass(s, a)

        wg = [held([P, S], F32, "wg%d" % t) for t in range(4)]
        for c in range(4):
            nc.tensor.transpose(banks[4][:, P * c : P * (c + 1)], wgs_raw[:, P * c : P * (c + 1)], ident[:])
        by_t = banks[4][:].rearrange("p (c g t i) -> p t c g i", c=4, g=4, t=4)
        spread = [h_own[0][:], h_own[1][:], h_own[2][:], as_f32(stages[1])]
        for t in range(4):
            nc.scalar.copy(
                spread[t].rearrange("p (c u g i) -> p c u g i", c=4, u=4, g=4),
                by_t[:, t].unsqueeze(2).to_broadcast([P, 4, 4, 4, 8]),
            )
            back = banks[5 + t % 3]
            for c in range(4):
                nc.tensor.transpose(back[:, P * c : P * (c + 1)], spread[t][:, P * c : P * (c + 1)], ident[:])
            nc.scalar.copy(wg[t][:], back[:])

        nc.vector.tensor_copy(v_words[0][:], tab[0][:].indirect(idx[:]))
        nc.vector.tensor_copy(
            w4_codes[:].bitcast(I32).rearrange("p a (b t g w) -> p (a b) t g w", b=HB, t=4, g=16),
            w4_raw[:].bitcast(I32).rearrange("p a (b g t w) -> p (a b) t g w", b=HB, t=4, g=16),
        )
        quant_w1(0, 0, stages[0], False)

        nc.vector.tensor_copy(v_words[1][:], tab[1][:].indirect(idx[:]))
        quant_w1(1, 0, stages[1], False)
        nc.vector.tensor_copy(v_words[2][:], tab[2][:].indirect(idx[:]))
        for a in range(KA - 1):
            for s in range(2):
                w4_pass(s, a)
                w1_pass(s, a)
        w4_pass(0, KA - 1)
        quant_w1(2, 0, stages[1], True)
        w1_pass(0, KA - 1)
        w4_pass(1, KA - 1)
        w1_pass(1, KA - 1)

        course_raw = [held([P, 4 * R], F32, "craw%d" % b, "big%d" % b) for b in range(HB)]
        for b in range(HB):
            for t in range(4):
                nc.sync.dma_start(course_raw[b][:, R * t : R * (t + 1)], course_rows[b, t])

        def weave(engine_copy, dst, src):
            engine_copy(dst.rearrange("p (c i t) -> p c t i", i=4, t=4), src.rearrange("p t (c i) -> p c t i", i=4))

        page_codes = [held([P, T2], U32, "pc%d" % b) for b in range(HB)]
        page_sc = [held([P, T2], U8, "ps%d" % b) for b in range(HB)]
        course_codes = [held([P, R], U32, "cc%d" % b) for b in range(HB)]
        course_sc = [held([P, R], U8, "cs%d" % b) for b in range(HB)]
        page_bf = [
            raw[:].bitcast(BF16).rearrange("p (t m) -> p t m", t=4) for raw in (w1_raw[2, 1], course_raw[1])
        ]

        features = [h_own[1][:], stages[2][:, 1024:2048].bitcast(F32), h_own[0][:]]
        features = features + [as_f32(stages[2])]
        features = features + [features[3], h_own[2][:], h_own[0][:], w1_raw[2, 1][:, 0:S]]

        def add_up(s):
            nc.vector.tensor_tensor(in_four(features[s]), in_four(banks[w1_bank[s]][:]), sizes[s], ALU.add)

        def put(s):
            nc.vector.tensor_tensor(page[s][:].indirect(idx2[:]), features[s], wg[s % 4][:], ALU.mult)

        def round_page(s):
            nc.scalar.copy(page_bf[s // 4][:, s % 4, :], page[s][:])

        def quant_course(b, stage):
            weave(nc.scalar.copy, stage, course_raw[b][:].rearrange("p (t j) -> p t j", t=4))
            quantize(course_codes[b][:], course_sc[b][:], stage)

        halves = [held([P, 2048], BF16, "half%d" % n) for n in range(2)]
        course_stage = [w1_raw[2, 1][:, 1024 * b : 1024 * (b + 1)].bitcast(BF16) for b in range(HB)]
        add_up(0)
        put(0)
        add_up(1)
        put(1)
        products(2)
        add_up(2)
        put(2)
        products(3)
        for a in range(2):
            quant_w1(a, 1, late_stages[a], False)
        quant_w1(2, 1, stages[2], False)
        add_up(3)
        put(3)
        products(4)
        products(5)
        nc.tensor.transpose(banks[3][:, 0:P], vec_rows[:], ident[:])
        vec_cols = held([P, 32], F32, "vec_cols")
        nc.scalar.copy(vec_cols[:], banks[3][:, 0:32])
        products(6)
        add_up(4)
        products(7)
        add_up(5)
        put(4)
        add_up(6)
        put(5)
        put(6)
        for s in range(4):
            round_page(s)
        for u in range(2):
            cols = slice(512 * u, 512 * (u + 1))
            weave(nc.scalar.copy, halves[u][:], page_bf[0][:, :, cols])
            quantize(page_codes[0][:, cols], page_sc[0][:, cols], halves[u][:])
        quant_course(0, course_stage[0])
        add_up(7)
        quant_course(1, course_stage[1])
        put(7)
        for s in range(4, 8):
            round_page(s)

        def stage_two(acc, n, codes, scales):
            cols = slice(P * n, P * (n + 1))
            for b in range(HB):
                nc.tensor.matmul_mx(
                    acc[:],
                    lhsT=page_codes[b][:, cols].bitcast(FP8X4),
                    lhsT_scale=page_sc[b][:, cols],
                    rhs=codes[b][:].bitcast(FP8X4),
                    rhs_scale=scales[b][:],
                    start=(b == 0),
                    stop=(b == HB - 1),
                )

        x_codes = [held([P, R], U32, "xc%d" % b) for b in range(HB)]
        x_sc = [held([P, R], U8, "xs%d" % b) for b in range(HB)]
        x_space = held([P, 3 * 1024], BF16, "x_space")
        x_flat = [halves[0][:], x_space[:, 0:2048]]
        x_bf = [flat.rearrange("p (t j) -> p t j", t=4) for flat in x_flat]
        damp = [w1_raw[n // 4, 1][:, R * (n % 4) : R * (n % 4 + 1)] for n in range(MT)]
        quarters = [held([P, 1024], BF16, "quarter%d" % c) for c in range(4)]
        x_woven = [x_space[:, 1024:3072], halves[1][:]]
        roots = [held([P, R], F32, "root%d" % n) for n in range(2)]

        def pick(s, picked):
            nc.vector.tensor_copy(picked, page[s][:].indirect(idx3[:]))

        def rate_rivals(s, picked):
            nc.vector.tensor_scalar(
                x_bf[s // 4][:, s % 4, :], picked, vec_cols[:, 8 + s : 9 + s], vec_cols[:, 16 + s : 17 + s], ALU.max, ALU.mult
            )

        def damp_size(n, size):
            acc = banks[(4 + n) % 8]
            stage_two(acc, n, course_codes, course_sc)
            nc.scalar.activation(size, acc[:], ACT.Abs)

        def damp_root(size, root):
            nc.scalar.activation(root, size, ACT.Abs_reciprocal_sqrt, bias=1.0)

        def damp_square(n, root):
            nc.scalar.activation(damp[n], root, ACT.Square)

        def damping(n, size, root):
            damp_size(n, size)
            damp_root(size, root)
            damp_square(n, root)

        picked = [features[7]] + [as_f32(quarter) for quarter in quarters]
        picked = picked + picked[1:4]
        for c in range(4):
            pick(c, picked[c])
            cols = slice(256 * c, 256 * (c + 1))
            weave(nc.vector.tensor_copy if c == 0 else nc.scalar.copy, quarters[c][:], page_bf[1][:, :, cols])
            if c == 0:
                rate_rivals(c, picked[c])
            quantize(page_codes[1][:, cols], page_sc[1][:, cols], quarters[c][:])
            if c > 0:
                rate_rivals(c, picked[c])
        for s in range(4, 8):
            pick(s, picked[s])
        for s in (4, 5):
            rate_rivals(s, picked[s])
        damping(0, spare[0], roots[0][:])
        damping(1, spare[1], roots[1][:])
        damping(2, spare[2], as_f32(x_woven[0]))
        weave(nc.scalar.copy, x_woven[0], x_bf[0])
        quantize(x_codes[0][:], x_sc[0][:], x_woven[0])
        for s in (6, 7):
            rate_rivals(s, picked[s])
        damping(3, spare[3], roots[0][:])
        damping(4, spare[0], x_woven[1][:, 1024:2048].bitcast(F32))
        weave(nc.vector.tensor_copy, x_woven[1][:, 0:1024], x_bf[1][:, :, 0:256])
        weave(nc.scalar.copy, x_woven[1][:, 1024:2048], x_bf[1][:, :, 256:R])
        for cols in (slice(0, 256), slice(256, R)):
            quantize(x_codes[1][:, cols], x_sc[1][:, cols], x_woven[1][:, 4 * cols.start : 4 * cols.stop])
        late = [x_flat[1][:, 1024 * u : 1024 * (u + 1)].bitcast(F32) for u in range(2)]
        for step in range(5, MT + 2):
            if step - 2 >= 5:
                damp_square(step - 2, roots[step % 2][:])
            if 5 <= step - 1 < MT:
                damp_root(late[(step - 1) % 2], roots[(step - 1) % 2][:])
            if step < MT:
                damp_size(step, late[step % 2])

        results = wg + h_own + [as_f32(stages[2])]
        for n in range(MT):
            acc = banks[(4 + n) % 8]
            stage_two(acc, n, x_codes, x_sc)
            res = results[n][:]
            nc.vector.scalar_tensor_tensor(res, acc[:], vec_cols[:, 24 + n : 25 + n], damp[n], ALU.mult, ALU.mult)
            nc.sync.dma_start(out[P * n : P * (n + 1), :], res)
